import numpy as np
import ml_dtypes


def mxq(x, axis, fmt="e4m3"):
    dtype, down = {"e4m3": (ml_dtypes.float8_e4m3fn, 7), "e5m2": (ml_dtypes.float8_e5m2, 14)}[fmt]
    v = np.moveaxis(np.asarray(x, np.float32).astype(ml_dtypes.bfloat16).astype(np.float64), axis, -1)
    blocks = v.reshape(v.shape[:-1] + (-1, 32))
    amax = np.abs(blocks).max(-1, keepdims=True)
    byte = np.maximum(np.where(amax > 0, np.frexp(amax)[1] - 1 + 127, 0) - down, 1)
    scale = np.exp2(byte - 127.0)
    codes = (blocks / scale).astype(np.float32).astype(dtype).astype(np.float64)
    return np.moveaxis((codes * scale).reshape(v.shape), -1, axis)


WIDE = False


def mx_kscale(k):
    if not WIDE:
        return np.ones(k)
    levels = np.array([30, -30])
    if k % 512:
        return np.exp2(np.random.permutation(np.resize(levels, k // 32))).repeat(32)
    a = np.empty((k // 512, 16))
    for p in range(k // 512):
        a[p, :8] = np.random.permutation(np.resize(levels, 8))
        for g in range(8):
            far = levels[np.abs(levels - a[p, g]) >= 10]
            a[p, g + 8] = far[np.random.randint(len(far))]
    return np.exp2(a.ravel()).repeat(32)


def f64(x):
    return np.asarray(x).astype(np.float64)


def striped(idx):
    return np.tile(np.asarray(idx).reshape(-1, 16).T, (8, 1)).astype(np.uint16)


def unstriped(offs):
    return offs[:16].T.reshape(-1).astype(np.int64)


E2M1 = np.array([0.0, 0.5, 1.0, 1.5, 2.0, 3.0, 4.0, 6.0, -0.0, -0.5, -1.0, -1.5, -2.0, -3.0, -4.0, -6.0])


def pack_weight(w, fmt):
    k, n = w.shape
    w = f64(np.asarray(w, np.float32).astype(ml_dtypes.bfloat16)).reshape(k // 32, 32, n)
    amax = np.abs(w).max(1)
    if fmt in ("e4m3", "e5m2"):
        byte = np.frexp(amax)[1] - 1 + 127 - (7 if fmt == "e4m3" else 14)
    else:
        mant, ex = np.frexp(amax / 6.0)
        byte = np.where(mant > 0.5, ex, ex - 1) + 127
    byte = np.clip(np.where(amax > 0, byte, 1), 1, 254)
    scaled = (w * np.exp2(127.0 - byte)[:, None, :]).reshape(k, n).astype(np.float32)
    by_word = np.ascontiguousarray(scaled.reshape(k // 512, 128, 4, n).transpose(0, 1, 3, 2))
    if fmt in ("e4m3", "e5m2"):
        words = by_word.astype(ml_dtypes.float8_e4m3fn if fmt == "e4m3" else ml_dtypes.float8_e5m2).view(np.uint8)
    else:
        c = by_word.astype(ml_dtypes.float4_e2m1fn).view(np.uint8) & 0xF
        words = (c[..., 0::2] | (c[..., 1::2] << 4)).reshape(k // 512, 128, 2 * n)
    return np.ascontiguousarray(words), np.ascontiguousarray(byte.astype(np.uint8).reshape(k // 512, 16, n))


def unpack_weight(words, scales, fmt):
    g, _, n = scales.shape
    words = np.ascontiguousarray(words).reshape(g, 128, n, -1)
    if fmt in ("e4m3", "e5m2"):
        vals = words.view(ml_dtypes.float8_e4m3fn if fmt == "e4m3" else ml_dtypes.float8_e5m2).astype(np.float64)
    else:
        nib = np.empty((g, 128, n, 4), np.uint8)
        nib[..., 0::2] = words & 0xF
        nib[..., 1::2] = words >> 4
        vals = E2M1[nib]
    vals = vals * np.repeat(np.exp2(scales.astype(np.float64) - 127.0), 8, axis=1)[..., None]
    return vals.transpose(0, 1, 3, 2).reshape(g * 512, n)


K, T, J, N, G = 1024, 1024, 256, 256, 32


def setup_inputs():
    n = np.random.standard_normal
    idx = np.random.permutation(T)[:J]
    fk = mx_kscale(K)
    xtp = pack_weight(n((K, T)) * np.random.uniform(0.4, 1.6, (1, T)) / fk[:, None], "e4m3")
    wap = pack_weight(n((K, N)) * 1 / np.sqrt(K) * fk[:, None], "e5m2")
    return {
        "xt_words": xtp[0],
        "xt_scales": xtp[1],
        "wa_words": wap[0],
        "wa_scales": wap[1],
        "wb": (n((K, N)) * 1 / np.sqrt(K) * fk[:, None]).astype(np.float32),
        "bi": (np.random.uniform(-0.6, 0.6, (1, N))).astype(np.float32),
        "offs": striped(idx),
    }


def reference(xt_words, xt_scales, wa_words, wa_scales, wb, bi, offs):
    idx = unstriped(offs)
    xtu = unpack_weight(xt_words, xt_scales, "e4m3")
    wau = unpack_weight(wa_words, wa_scales, "e5m2")
    xtidxg = xtu[:, idx]
    a = xtidxg.T @ wau
    wbq = mxq(f64(wb), 0, "e5m2")
    b0 = xtidxg.T @ wbq
    b2 = b0 + f64(bi)
    g1 = a.reshape(J, G, N // G).mean(axis=2)
    g2 = np.repeat(g1, N // G, axis=1)
    y = (a - g2) * np.abs(b2)
    return y

@@ -1,0 +1,185 @@
+from contextlib import ExitStack
+
+import concourse.mybir as mybir
+
+K, T, J, N, G = 1024, 1024, 256, 256, 32
+FLOPS = 2 * 2 * J * K * N
+
+F32 = mybir.dt.float32
+BF16 = mybir.dt.bfloat16
+I32 = mybir.dt.int32
+U32 = mybir.dt.uint32
+U16 = mybir.dt.uint16
+U8 = mybir.dt.uint8
+E4M3 = mybir.dt.float8_e4m3fn_x4
+E5M2 = mybir.dt.float8_e5m2_x4
+ALU = mybir.AluOpType
+ACT = mybir.ActivationFunctionType
+
+P = 128
+PACK = 4
+PASSES = K // (P * PACK)
+HALVES = 2
+GROUP = N // G
+QUAD = 32
+SCALE_ROWS = 4
+
+
+def tile_list_rows_onetoken_groupcentred_kernel(tc, xt_words, xt_scales, wa_words, wa_scales, wb, bi, offs, out):
+    nc = tc.nc
+    with ExitStack() as ctx:
+        sb = ctx.enter_context(tc.tile_pool(name="sb", bufs=1))
+        ps = ctx.enter_context(tc.psum_pool(name="ps", bufs=1))
+
+        offsets = sb.tile([P, J // 16], U16, name="offsets")
+        x_words = [sb.tile([P, T], U32, name=f"x_words{z}", align_bytes=64) for z in range(PASSES)]
+        x_scales = sb.tile([P, PASSES, T], U8, name="x_scales", align_bytes=64)
+        a_words = sb.tile([P, PASSES, N], U32, name="a_words", align_bytes=64)
+        a_scales = sb.tile([P, PASSES, N], U8, name="a_scales", align_bytes=64)
+        b_raw = [sb.tile([P, PACK, N], F32, name=f"b_raw{z}", tag=f"raw{z}", align_bytes=64) for z in range(PASSES)]
+        bias_runs = sb.tile([P, N // QUAD], F32, name="bias_runs", align_bytes=64)
+
+        nc.gpsimd.memset(x_scales[:, 0, :].bitcast(I32), 0)
+        nc.vector.memset(x_scales[:, 1, :].bitcast(I32), 0)
+        nc.vector.memset(a_scales[:].bitcast(I32), 0)
+
+        def load_scale_rows(plane, scales):
+            rows = scales.rearrange("z (q r) c -> r q z c", r=SCALE_ROWS)
+            for r in range(SCALE_ROWS):
+                nc.sync.dma_start(out=plane[r:P:QUAD, :, :].bitcast(I32), in_=rows[r].bitcast(I32))
+
+        def load_x_words(z):
+            nc.sync.dma_start(out=x_words[z][:].bitcast(I32), in_=xt_words[z].rearrange("p c t -> p (c t)").bitcast(I32))
+
+        def load_wb(z, queue):
+            rows = wb[z * P * PACK : (z + 1) * P * PACK, :]
+            queue.dma_start(out=b_raw[z][:], in_=rows.rearrange("(p t) n -> p t n", t=PACK))
+
+        nc.sync.dma_start(offsets[:], offs)
+        load_wb(0, nc.scalar)
+        nc.sync.dma_start(
+            out=bias_runs[:], in_=bi.rearrange("o (j b) -> o j b", j=QUAD).to_broadcast([P // QUAD, QUAD, N // QUAD])
+        )
+        load_scale_rows(x_scales, xt_scales)
+        load_x_words(0)
+        load_x_words(1)
+        nc.sync.dma_start(out=a_words[:].bitcast(I32), in_=wa_words.rearrange("z p c t -> p z (c t)").bitcast(I32))
+        load_scale_rows(a_scales, wa_scales)
+        load_wb(1, nc.sync)
+
+        repeated = sb.tile([P, N // QUAD, QUAD], F32, name="repeated", align_bytes=64)
+        nc.scalar.copy(out=repeated[:], in_=bias_runs[:].unsqueeze(2).to_broadcast([P, N // QUAD, QUAD]))
+        turned = sb.tile([P, N // QUAD, QUAD], F32, name="turned", align_bytes=64)
+        nc.vector.transpose(turned[:].rearrange("p b j -> p (b j)"), repeated[:].rearrange("p b i -> p (b i)"))
+        bias = sb.tile([P, N], F32, name="bias")
+        nc.scalar.copy(out=bias[:].rearrange("p (j b) -> p j b", j=QUAD), in_=turned[:].rearrange("p b j -> p j b"))
+
+        def interleaved(dst):
+            return dst.rearrange("p (c i) t -> p c t i", i=4)
+
+        def by_row(src):
+            return src.rearrange("p t (c i) -> p c t i", i=4)
+
+        b_words = {}
+        b_scales = {}
+        rounded0 = sb.tile([P, N, PACK], BF16, name="rounded0", align_bytes=64)
+        nc.scalar.activation(out=interleaved(rounded0[:]), in_=by_row(b_raw[0][:]), func=ACT.Copy)
+
+        g_words = [sb.tile([P, J], U32, name=f"g_words{z}", align_bytes=64) for z in range(PASSES)]
+        g_scales = [sb.tile([P, J], U8, name=f"g_scales{z}", align_bytes=64) for z in range(PASSES)]
+        for z in range(PASSES):
+            nc.vector.tensor_copy(g_scales[z][:], x_scales[:, z, :].indirect(offsets[:]))
+        nc.vector.tensor_copy(g_words[0][:], x_words[0][:].indirect(offsets[:]))
+        words0 = sb.tile([P, N], U32, name="b_words0", align_bytes=64)
+        scales0 = sb.tile([P, N], U8, name="b_scales0", align_bytes=64)
+        nc.vector.quantize_mx(out=words0[:].bitcast(E5M2), scales=scales0[:], in_=rounded0[:].rearrange("p c t -> p (c t)"))
+        for h in range(HALVES):
+            b_words[0, h] = words0[:, h * P : (h + 1) * P]
+            b_scales[0, h] = scales0[:, h * P : (h + 1) * P]
+        nc.vector.tensor_copy(g_words[1][:], x_words[1][:].indirect(offsets[:]))
+
+        b_bank = [ps.tile([P, HALVES, P], F32, name=f"b_bank{h}") for h in range(HALVES)]
+
+        def multiply_b(z, h):
+            for u in range(HALVES):
+                tokens = slice(u * P, (u + 1) * P)
+                nc.tensor.matmul_mx(
+                    out=b_bank[h][:, u, :],
+                    lhsT=g_words[z][:, tokens].bitcast(E4M3),
+                    lhsT_scale=g_scales[z][:, tokens],
+                    rhs=b_words[z, h].bitcast(E5M2),
+                    rhs_scale=b_scales[z, h],
+                    start=(z == 0 and u == 0),
+                    stop=(z == PASSES - 1 and u == HALVES - 1),
+                )
+
+        for h in range(HALVES):
+            multiply_b(0, h)
+
+        a_bank = [ps.tile([P, N], F32, name=f"a_bank{h}") for h in range(HALVES)]
+        for h in range(HALVES):
+            tokens = slice(h * P, (h + 1) * P)
+            for z in range(PASSES):
+                nc.tensor.matmul_mx(
+                    out=a_bank[h][:],
+                    lhsT=g_words[z][:, tokens].bitcast(E4M3),
+                    lhsT_scale=g_scales[z][:, tokens],
+                    rhs=a_words[:, z, :].bitcast(E5M2),
+                    rhs_scale=a_scales[:, z, :],
+                    start=(z == 0),
+                    stop=(z == PASSES - 1),
+                )
+        def group_sums(h, sums):
+            nc.vector.tensor_reduce(
+                out=sums,
+                in_=a_bank[h][:].rearrange("p (g i) -> p g i", i=GROUP),
+                axis=mybir.AxisListType.X,
+                op=ALU.add,
+            )
+
+        sums0 = sb.tile([P, G], F32, name="sums0", align_bytes=64)
+        group_sums(0, sums0[:])
+
+        rounded1 = sb.tile([P, N, PACK], BF16, name="rounded1", tag="rounded_then_centred", align_bytes=64)
+        nc.vector.tensor_copy(out=interleaved(rounded1[:, 0:P, :]), in_=by_row(b_raw[1][:, :, 0:P]))
+        nc.scalar.activation(out=interleaved(rounded1[:, P:N, :]), in_=by_row(b_raw[1][:, :, P:N]), func=ACT.Copy)
+        for h in range(HALVES):
+            words1 = sb.tile([P, P], U32, name=f"b_words1_{h}", align_bytes=64)
+            scales1 = sb.tile([P, P], U8, name=f"b_scales1_{h}", align_bytes=64)
+            nc.vector.quantize_mx(
+                out=words1[:].bitcast(E5M2),
+                scales=scales1[:],
+                in_=rounded1[:, h * P : (h + 1) * P, :].rearrange("p c t -> p (c t)"),
+            )
+            b_words[1, h] = words1[:]
+            b_scales[1, h] = scales1[:]
+
+        sums1 = sb.tile([P, G], F32, name="sums1", tag="raw1", align_bytes=64)
+        group_sums(1, sums1[:])
+        centred = sb.tile([P, HALVES, N], F32, name="centred", tag="rounded_then_centred", align_bytes=64)
+        for h, sums in enumerate((sums0, sums1)):
+            nc.vector.scalar_tensor_tensor(
+                out=centred[:, h, :].rearrange("p (g i) -> p g i", i=GROUP),
+                in0=sums[:].unsqueeze(2).to_broadcast([P, G, GROUP]),
+                scalar=-1.0 / GROUP,
+                in1=a_bank[h][:].rearrange("p (g i) -> p g i", i=GROUP),
+                op0=ALU.mult,
+                op1=ALU.add,
+            )
+
+        for h in range(HALVES):
+            multiply_b(1, h)
+        out_view = out.rearrange("(u p) n -> p u n", p=P)
+        biased = [sb.tile([P, HALVES, P], F32, name=f"biased{h}", align_bytes=64) for h in range(HALVES)]
+        size = [sb.tile([P, HALVES, P], F32, name=f"size{h}", align_bytes=64) for h in range(HALVES)]
+        for h in range(HALVES):
+            cols = slice(h * P, (h + 1) * P)
+            nc.vector.tensor_tensor(
+                out=biased[h][:], in0=b_bank[h][:], in1=bias[:, cols].unsqueeze(1).to_broadcast([P, HALVES, P]), op=ALU.add
+            )
+            nc.scalar.activation(out=size[h][:], in_=biased[h][:], func=ACT.Abs)
+        for h in range(HALVES):
+            cols = slice(h * P, (h + 1) * P)
+            result = sb.tile([P, HALVES, P], F32, name=f"result{h}", align_bytes=64)
+            nc.vector.tensor_tensor(out=result[:], in0=size[h][:], in1=centred[:, :, cols], op=ALU.mult)
+            nc.sync.dma_start(out=out_view[:, :, cols], in_=result[:])

@@ -36,7 +36,7 @@ def tile_list_rows_onetoken_groupcentred_kernel(tc, xt_words, xt_scales, wa_word
         x_scales = sb.tile([P, PASSES, T], U8, name="x_scales", align_bytes=64)
         a_words = sb.tile([P, PASSES, N], U32, name="a_words", align_bytes=64)
         a_scales = sb.tile([P, PASSES, N], U8, name="a_scales", align_bytes=64)
-        b_raw = [sb.tile([P, PACK, N], F32, name=f"b_raw{z}", tag=f"raw{z}", align_bytes=64) for z in range(PASSES)]
+        b_raw = [sb.tile([P, PACK, N], F32, name=f"b_raw{z}", align_bytes=64) for z in range(PASSES)]
         bias_runs = sb.tile([P, N // QUAD], F32, name="bias_runs", align_bytes=64)
 
         nc.gpsimd.memset(x_scales[:, 0, :].bitcast(I32), 0)
@@ -48,23 +48,23 @@ def tile_list_rows_onetoken_groupcentred_kernel(tc, xt_words, xt_scales, wa_word
             for r in range(SCALE_ROWS):
                 nc.sync.dma_start(out=plane[r:P:QUAD, :, :].bitcast(I32), in_=rows[r].bitcast(I32))
 
-        def load_x_words(z):
-            nc.sync.dma_start(out=x_words[z][:].bitcast(I32), in_=xt_words[z].rearrange("p c t -> p (c t)").bitcast(I32))
+        def load_x_words(z, queue):
+            queue.dma_start(out=x_words[z][:].bitcast(I32), in_=xt_words[z].rearrange("p c t -> p (c t)").bitcast(I32))
 
         def load_wb(z, queue):
             rows = wb[z * P * PACK : (z + 1) * P * PACK, :]
             queue.dma_start(out=b_raw[z][:], in_=rows.rearrange("(p t) n -> p t n", t=PACK))
 
         nc.sync.dma_start(offsets[:], offs)
-        load_wb(0, nc.scalar)
+        load_x_words(0, nc.scalar)
         nc.sync.dma_start(
             out=bias_runs[:], in_=bi.rearrange("o (j b) -> o j b", j=QUAD).to_broadcast([P // QUAD, QUAD, N // QUAD])
         )
         load_scale_rows(x_scales, xt_scales)
-        load_x_words(0)
-        load_x_words(1)
+        load_x_words(1, nc.sync)
         nc.sync.dma_start(out=a_words[:].bitcast(I32), in_=wa_words.rearrange("z p c t -> p z (c t)").bitcast(I32))
         load_scale_rows(a_scales, wa_scales)
+        load_wb(0, nc.sync)
         load_wb(1, nc.sync)
 
         repeated = sb.tile([P, N // QUAD, QUAD], F32, name="repeated", align_bytes=64)
@@ -80,48 +80,18 @@ def tile_list_rows_onetoken_groupcentred_kernel(tc, xt_words, xt_scales, wa_word
         def by_row(src):
             return src.rearrange("p t (c i) -> p c t i", i=4)
 
-        b_words = {}
-        b_scales = {}
-        rounded0 = sb.tile([P, N, PACK], BF16, name="rounded0", align_bytes=64)
-        nc.scalar.activation(out=interleaved(rounded0[:]), in_=by_row(b_raw[0][:]), func=ACT.Copy)
-
         g_words = [sb.tile([P, J], U32, name=f"g_words{z}", align_bytes=64) for z in range(PASSES)]
         g_scales = [sb.tile([P, J], U8, name=f"g_scales{z}", align_bytes=64) for z in range(PASSES)]
         for z in range(PASSES):
             nc.vector.tensor_copy(g_scales[z][:], x_scales[:, z, :].indirect(offsets[:]))
-        nc.vector.tensor_copy(g_words[0][:], x_words[0][:].indirect(offsets[:]))
-        words0 = sb.tile([P, N], U32, name="b_words0", align_bytes=64)
-        scales0 = sb.tile([P, N], U8, name="b_scales0", align_bytes=64)
-        nc.vector.quantize_mx(out=words0[:].bitcast(E5M2), scales=scales0[:], in_=rounded0[:].rearrange("p c t -> p (c t)"))
-        for h in range(HALVES):
-            b_words[0, h] = words0[:, h * P : (h + 1) * P]
-            b_scales[0, h] = scales0[:, h * P : (h + 1) * P]
-        nc.vector.tensor_copy(g_words[1][:], x_words[1][:].indirect(offsets[:]))
+            nc.vector.tensor_copy(g_words[z][:], x_words[z][:].indirect(offsets[:]))
 
-        b_bank = [ps.tile([P, HALVES, P], F32, name=f"b_bank{h}") for h in range(HALVES)]
-
-        def multiply_b(z, h):
+        a_bank = [ps.tile([P, N], F32, name=f"a_bank{u}") for u in range(HALVES)]
+        for z in range(PASSES):
             for u in range(HALVES):
                 tokens = slice(u * P, (u + 1) * P)
                 nc.tensor.matmul_mx(
-                    out=b_bank[h][:, u, :],
-                    lhsT=g_words[z][:, tokens].bitcast(E4M3),
-                    lhsT_scale=g_scales[z][:, tokens],
-                    rhs=b_words[z, h].bitcast(E5M2),
-                    rhs_scale=b_scales[z, h],
-                    start=(z == 0 and u == 0),
-                    stop=(z == PASSES - 1 and u == HALVES - 1),
-                )
-
-        for h in range(HALVES):
-            multiply_b(0, h)
-
-        a_bank = [ps.tile([P, N], F32, name=f"a_bank{h}") for h in range(HALVES)]
-        for h in range(HALVES):
-            tokens = slice(h * P, (h + 1) * P)
-            for z in range(PASSES):
-                nc.tensor.matmul_mx(
-                    out=a_bank[h][:],
+                    out=a_bank[u][:],
                     lhsT=g_words[z][:, tokens].bitcast(E4M3),
                     lhsT_scale=g_scales[z][:, tokens],
                     rhs=a_words[:, z, :].bitcast(E5M2),
@@ -129,46 +99,61 @@ def tile_list_rows_onetoken_groupcentred_kernel(tc, xt_words, xt_scales, wa_word
                     start=(z == 0),
                     stop=(z == PASSES - 1),
                 )
-        def group_sums(h, sums):
+        sums = sb.tile([P, HALVES, G], F32, name="sums", align_bytes=64)
+        centred = sb.tile([P, HALVES, N], F32, name="centred", align_bytes=64)
+        for u in range(HALVES):
             nc.vector.tensor_reduce(
-                out=sums,
-                in_=a_bank[h][:].rearrange("p (g i) -> p g i", i=GROUP),
+                out=sums[:, u, :],
+                in_=a_bank[u][:].rearrange("p (g i) -> p g i", i=GROUP),
                 axis=mybir.AxisListType.X,
                 op=ALU.add,
             )
 
-        sums0 = sb.tile([P, G], F32, name="sums0", align_bytes=64)
-        group_sums(0, sums0[:])
-
-        rounded1 = sb.tile([P, N, PACK], BF16, name="rounded1", tag="rounded_then_centred", align_bytes=64)
-        nc.vector.tensor_copy(out=interleaved(rounded1[:, 0:P, :]), in_=by_row(b_raw[1][:, :, 0:P]))
-        nc.scalar.activation(out=interleaved(rounded1[:, P:N, :]), in_=by_row(b_raw[1][:, :, P:N]), func=ACT.Copy)
-        for h in range(HALVES):
-            words1 = sb.tile([P, P], U32, name=f"b_words1_{h}", align_bytes=64)
-            scales1 = sb.tile([P, P], U8, name=f"b_scales1_{h}", align_bytes=64)
-            nc.vector.quantize_mx(
-                out=words1[:].bitcast(E5M2),
-                scales=scales1[:],
-                in_=rounded1[:, h * P : (h + 1) * P, :].rearrange("p c t -> p (c t)"),
-            )
-            b_words[1, h] = words1[:]
-            b_scales[1, h] = scales1[:]
-
-        sums1 = sb.tile([P, G], F32, name="sums1", tag="raw1", align_bytes=64)
-        group_sums(1, sums1[:])
-        centred = sb.tile([P, HALVES, N], F32, name="centred", tag="rounded_then_centred", align_bytes=64)
-        for h, sums in enumerate((sums0, sums1)):
+        def centre(u):
             nc.vector.scalar_tensor_tensor(
-                out=centred[:, h, :].rearrange("p (g i) -> p g i", i=GROUP),
-                in0=sums[:].unsqueeze(2).to_broadcast([P, G, GROUP]),
+                out=centred[:, u, :].rearrange("p (g i) -> p g i", i=GROUP),
+                in0=sums[:, u, :].unsqueeze(2).to_broadcast([P, G, GROUP]),
                 scalar=-1.0 / GROUP,
-                in1=a_bank[h][:].rearrange("p (g i) -> p g i", i=GROUP),
+                in1=a_bank[u][:].rearrange("p (g i) -> p g i", i=GROUP),
                 op0=ALU.mult,
                 op1=ALU.add,
             )
 
-        for h in range(HALVES):
-            multiply_b(1, h)
+        centre(0)
+
+        b_bank = [ps.tile([P, HALVES, P], F32, name=f"b_bank{h}") for h in range(HALVES)]
+        for z in range(PASSES):
+            rounded = []
+            for h in range(HALVES):
+                if z == PASSES - 1 and h == HALVES - 1:
+                    rounded.append(centred[:, 1, :].bitcast(BF16).rearrange("p (c t) -> p c t", t=PACK))
+                else:
+                    rounded.append(sb.tile([P, P, PACK], BF16, name=f"rounded{z}_{h}", align_bytes=64)[:])
+            for h in range(HALVES):
+                src = by_row(b_raw[z][:, :, h * P : (h + 1) * P])
+                if z == PASSES - 1 and h == 0:
+                    nc.vector.tensor_copy(out=interleaved(rounded[h]), in_=src)
+                else:
+                    nc.scalar.activation(out=interleaved(rounded[h]), in_=src, func=ACT.Copy)
+            for h in range(HALVES):
+                b_words = sb.tile([P, P], U32, name=f"b_words{z}_{h}", align_bytes=64)
+                b_scales = sb.tile([P, P], U8, name=f"b_scales{z}_{h}", align_bytes=64)
+                nc.vector.quantize_mx(
+                    out=b_words[:].bitcast(E5M2), scales=b_scales[:], in_=rounded[h].rearrange("p c t -> p (c t)")
+                )
+                for u in range(HALVES):
+                    tokens = slice(u * P, (u + 1) * P)
+                    nc.tensor.matmul_mx(
+                        out=b_bank[h][:, u, :],
+                        lhsT=g_words[z][:, tokens].bitcast(E4M3),
+                        lhsT_scale=g_scales[z][:, tokens],
+                        rhs=b_words[:].bitcast(E5M2),
+                        rhs_scale=b_scales[:],
+                        start=(z == 0 and u == 0),
+                        stop=(z == PASSES - 1 and u == HALVES - 1),
+                    )
+
+        centre(1)
         out_view = out.rearrange("(u p) n -> p u n", p=P)
         biased = [sb.tile([P, HALVES, P], F32, name=f"biased{h}", align_bytes=64) for h in range(HALVES)]
         size = [sb.tile([P, HALVES, P], F32, name=f"size{h}", align_bytes=64) for h in range(HALVES)]

@@ -37,16 +37,16 @@ def tile_list_rows_onetoken_groupcentred_kernel(tc, xt_words, xt_scales, wa_word
         a_words = sb.tile([P, PASSES, N], U32, name="a_words", align_bytes=64)
         a_scales = sb.tile([P, PASSES, N], U8, name="a_scales", align_bytes=64)
         b_raw = [sb.tile([P, PACK, N], F32, name=f"b_raw{z}", align_bytes=64) for z in range(PASSES)]
-        bias_runs = sb.tile([P, N // QUAD], F32, name="bias_runs", align_bytes=64)
+        bias_row = sb.tile([P, N], F32, name="bias_row", align_bytes=64)
 
-        nc.gpsimd.memset(x_scales[:, 0, :].bitcast(I32), 0)
-        nc.vector.memset(x_scales[:, 1, :].bitcast(I32), 0)
-        nc.vector.memset(a_scales[:].bitcast(I32), 0)
+        nc.gpsimd.memset(bias_row[:], 0.0)
+        nc.vector.memset(x_scales[:].bitcast(I32), 0)
+        nc.gpsimd.memset(a_scales[:].bitcast(I32), 0)
 
-        def load_scale_rows(plane, scales):
+        def load_scale_rows(plane, scales, queues):
             rows = scales.rearrange("z (q r) c -> r q z c", r=SCALE_ROWS)
             for r in range(SCALE_ROWS):
-                nc.sync.dma_start(out=plane[r:P:QUAD, :, :].bitcast(I32), in_=rows[r].bitcast(I32))
+                queues[r % len(queues)].dma_start(out=plane[r:P:QUAD, :, :].bitcast(I32), in_=rows[r].bitcast(I32))
 
         def load_x_words(z, queue):
             queue.dma_start(out=x_words[z][:].bitcast(I32), in_=xt_words[z].rearrange("p c t -> p (c t)").bitcast(I32))
@@ -56,23 +56,21 @@ def tile_list_rows_onetoken_groupcentred_kernel(tc, xt_words, xt_scales, wa_word
             queue.dma_start(out=b_raw[z][:], in_=rows.rearrange("(p t) n -> p t n", t=PACK))
 
         nc.sync.dma_start(offsets[:], offs)
-        load_x_words(0, nc.scalar)
-        nc.sync.dma_start(
-            out=bias_runs[:], in_=bi.rearrange("o (j b) -> o j b", j=QUAD).to_broadcast([P // QUAD, QUAD, N // QUAD])
-        )
-        load_scale_rows(x_scales, xt_scales)
+        nc.scalar.dma_start(out=bias_row[0:P:QUAD, :], in_=bi.to_broadcast([P // QUAD, N]))
+        load_scale_rows(x_scales, xt_scales, (nc.sync, nc.scalar))
+        load_x_words(0, nc.sync)
         load_x_words(1, nc.sync)
         nc.sync.dma_start(out=a_words[:].bitcast(I32), in_=wa_words.rearrange("z p c t -> p z (c t)").bitcast(I32))
-        load_scale_rows(a_scales, wa_scales)
+        load_scale_rows(a_scales, wa_scales, (nc.sync,))
         load_wb(0, nc.sync)
         load_wb(1, nc.sync)
 
+        bias_cols = sb.tile([P, N // QUAD, QUAD], F32, name="bias_cols", align_bytes=64)
+        nc.vector.transpose(bias_cols[:].rearrange("p b j -> p (b j)"), bias_row[:])
         repeated = sb.tile([P, N // QUAD, QUAD], F32, name="repeated", align_bytes=64)
-        nc.scalar.copy(out=repeated[:], in_=bias_runs[:].unsqueeze(2).to_broadcast([P, N // QUAD, QUAD]))
-        turned = sb.tile([P, N // QUAD, QUAD], F32, name="turned", align_bytes=64)
-        nc.vector.transpose(turned[:].rearrange("p b j -> p (b j)"), repeated[:].rearrange("p b i -> p (b i)"))
-        bias = sb.tile([P, N], F32, name="bias")
-        nc.scalar.copy(out=bias[:].rearrange("p (j b) -> p j b", j=QUAD), in_=turned[:].rearrange("p b j -> p j b"))
+        nc.scalar.copy(out=repeated[:], in_=bias_cols[:, :, 0:1].to_broadcast([P, N // QUAD, QUAD]))
+        bias = sb.tile([P, N], F32, name="bias", align_bytes=64)
+        nc.vector.transpose(bias[:], repeated[:].rearrange("p b i -> p (b i)"))
 
         def interleaved(dst):
             return dst.rearrange("p (c i) t -> p c t i", i=4)

from contextlib import ExitStack

import concourse.mybir as mybir

K, T, J, N, G = 1024, 1024, 256, 256, 32
FLOPS = 2 * 2 * J * K * N

F32 = mybir.dt.float32
BF16 = mybir.dt.bfloat16
I32 = mybir.dt.int32
U32 = mybir.dt.uint32
U16 = mybir.dt.uint16
U8 = mybir.dt.uint8
E4M3 = mybir.dt.float8_e4m3fn_x4
E5M2 = mybir.dt.float8_e5m2_x4
ALU = mybir.AluOpType
ACT = mybir.ActivationFunctionType

P = 128
PACK = 4
PASSES = K // (P * PACK)
HALVES = 2
GROUP = N // G
QUAD = 32
SCALE_ROWS = 4


def tile_list_rows_onetoken_groupcentred_kernel(tc, xt_words, xt_scales, wa_words, wa_scales, wb, bi, offs, out):
    nc = tc.nc
    with ExitStack() as ctx:
        sb = ctx.enter_context(tc.tile_pool(name="sb", bufs=1))
        ps = ctx.enter_context(tc.psum_pool(name="ps", bufs=1))

        offsets = sb.tile([P, J // 16], U16, name="offsets")
        x_words = [sb.tile([P, T], U32, name=f"x_words{z}", align_bytes=64) for z in range(PASSES)]
        x_scales = sb.tile([P, PASSES, T], U8, name="x_scales", align_bytes=64)
        a_words = sb.tile([P, PASSES, N], U32, name="a_words", align_bytes=64)
        a_scales = sb.tile([P, PASSES, N], U8, name="a_scales", align_bytes=64)
        b_raw = [sb.tile([P, PACK, N], F32, name=f"b_raw{z}", align_bytes=64) for z in range(PASSES)]
        bias_row = sb.tile([P, N], F32, name="bias_row", align_bytes=64)

        nc.gpsimd.memset(bias_row[:], 0.0)
        nc.vector.memset(x_scales[:].bitcast(I32), 0)
        nc.gpsimd.memset(a_scales[:].bitcast(I32), 0)

        def load_scale_rows(plane, scales, queues):
            rows = scales.rearrange("z (q r) c -> r q z c", r=SCALE_ROWS)
            for r in range(SCALE_ROWS):
                queues[r % len(queues)].dma_start(out=plane[r:P:QUAD, :, :].bitcast(I32), in_=rows[r].bitcast(I32))

        def load_x_words(z, queue):
            queue.dma_start(out=x_words[z][:].bitcast(I32), in_=xt_words[z].rearrange("p c t -> p (c t)").bitcast(I32))

        def load_wb(z, queue):
            rows = wb[z * P * PACK : (z + 1) * P * PACK, :]
            queue.dma_start(out=b_raw[z][:], in_=rows.rearrange("(p t) n -> p t n", t=PACK))

        nc.sync.dma_start(offsets[:], offs)
        nc.scalar.dma_start(out=bias_row[0:P:QUAD, :], in_=bi.to_broadcast([P // QUAD, N]))
        load_scale_rows(x_scales, xt_scales, (nc.sync, nc.scalar))
        load_x_words(0, nc.sync)
        load_x_words(1, nc.sync)
        nc.sync.dma_start(out=a_words[:].bitcast(I32), in_=wa_words.rearrange("z p c t -> p z (c t)").bitcast(I32))
        load_scale_rows(a_scales, wa_scales, (nc.sync,))
        load_wb(0, nc.sync)
        load_wb(1, nc.sync)

        bias_cols = sb.tile([P, N // QUAD, QUAD], F32, name="bias_cols", align_bytes=64)
        nc.vector.transpose(bias_cols[:].rearrange("p b j -> p (b j)"), bias_row[:])
        repeated = sb.tile([P, N // QUAD, QUAD], F32, name="repeated", align_bytes=64)
        nc.scalar.copy(out=repeated[:], in_=bias_cols[:, :, 0:1].to_broadcast([P, N // QUAD, QUAD]))
        bias = sb.tile([P, N], F32, name="bias", align_bytes=64)
        nc.vector.transpose(bias[:], repeated[:].rearrange("p b i -> p (b i)"))

        def interleaved(dst):
            return dst.rearrange("p (c i) t -> p c t i", i=4)

        def by_row(src):
            return src.rearrange("p t (c i) -> p c t i", i=4)

        g_words = [sb.tile([P, J], U32, name=f"g_words{z}", align_bytes=64) for z in range(PASSES)]
        g_scales = [sb.tile([P, J], U8, name=f"g_scales{z}", align_bytes=64) for z in range(PASSES)]
        for z in range(PASSES):
            nc.vector.tensor_copy(g_scales[z][:], x_scales[:, z, :].indirect(offsets[:]))
            nc.vector.tensor_copy(g_words[z][:], x_words[z][:].indirect(offsets[:]))

        a_bank = [ps.tile([P, N], F32, name=f"a_bank{u}") for u in range(HALVES)]
        for z in range(PASSES):
            for u in range(HALVES):
                tokens = slice(u * P, (u + 1) * P)
                nc.tensor.matmul_mx(
                    out=a_bank[u][:],
                    lhsT=g_words[z][:, tokens].bitcast(E4M3),
                    lhsT_scale=g_scales[z][:, tokens],
                    rhs=a_words[:, z, :].bitcast(E5M2),
                    rhs_scale=a_scales[:, z, :],
                    start=(z == 0),
                    stop=(z == PASSES - 1),
                )
        sums = sb.tile([P, HALVES, G], F32, name="sums", align_bytes=64)
        centred = sb.tile([P, HALVES, N], F32, name="centred", align_bytes=64)
        for u in range(HALVES):
            nc.vector.tensor_reduce(
                out=sums[:, u, :],
                in_=a_bank[u][:].rearrange("p (g i) -> p g i", i=GROUP),
                axis=mybir.AxisListType.X,
                op=ALU.add,
            )

        def centre(u):
            nc.vector.scalar_tensor_tensor(
                out=centred[:, u, :].rearrange("p (g i) -> p g i", i=GROUP),
                in0=sums[:, u, :].unsqueeze(2).to_broadcast([P, G, GROUP]),
                scalar=-1.0 / GROUP,
                in1=a_bank[u][:].rearrange("p (g i) -> p g i", i=GROUP),
                op0=ALU.mult,
                op1=ALU.add,
            )

        centre(0)

        b_bank = [ps.tile([P, HALVES, P], F32, name=f"b_bank{h}") for h in range(HALVES)]
        for z in range(PASSES):
            rounded = []
            for h in range(HALVES):
                if z == PASSES - 1 and h == HALVES - 1:
                    rounded.append(centred[:, 1, :].bitcast(BF16).rearrange("p (c t) -> p c t", t=PACK))
                else:
                    rounded.append(sb.tile([P, P, PACK], BF16, name=f"rounded{z}_{h}", align_bytes=64)[:])
            for h in range(HALVES):
                src = by_row(b_raw[z][:, :, h * P : (h + 1) * P])
                if z == PASSES - 1 and h == 0:
                    nc.vector.tensor_copy(out=interleaved(rounded[h]), in_=src)
                else:
                    nc.scalar.activation(out=interleaved(rounded[h]), in_=src, func=ACT.Copy)
            for h in range(HALVES):
                b_words = sb.tile([P, P], U32, name=f"b_words{z}_{h}", align_bytes=64)
                b_scales = sb.tile([P, P], U8, name=f"b_scales{z}_{h}", align_bytes=64)
                nc.vector.quantize_mx(
                    out=b_words[:].bitcast(E5M2), scales=b_scales[:], in_=rounded[h].rearrange("p c t -> p (c t)")
                )
                for u in range(HALVES):
                    tokens = slice(u * P, (u + 1) * P)
                    nc.tensor.matmul_mx(
                        out=b_bank[h][:, u, :],
                        lhsT=g_words[z][:, tokens].bitcast(E4M3),
                        lhsT_scale=g_scales[z][:, tokens],
                        rhs=b_words[:].bitcast(E5M2),
                        rhs_scale=b_scales[:],
                        start=(z == 0 and u == 0),
                        stop=(z == PASSES - 1 and u == HALVES - 1),
                    )

        centre(1)
        out_view = out.rearrange("(u p) n -> p u n", p=P)
        biased = [sb.tile([P, HALVES, P], F32, name=f"biased{h}", align_bytes=64) for h in range(HALVES)]
        size = [sb.tile([P, HALVES, P], F32, name=f"size{h}", align_bytes=64) for h in range(HALVES)]
        for h in range(HALVES):
            cols = slice(h * P, (h + 1) * P)
            nc.vector.tensor_tensor(
                out=biased[h][:], in0=b_bank[h][:], in1=bias[:, cols].unsqueeze(1).to_broadcast([P, HALVES, P]), op=ALU.add
            )
            nc.scalar.activation(out=size[h][:], in_=biased[h][:], func=ACT.Abs)
        for h in range(HALVES):
            cols = slice(h * P, (h + 1) * P)
            result = sb.tile([P, HALVES, P], F32, name=f"result{h}", align_bytes=64)
            nc.vector.tensor_tensor(out=result[:], in0=size[h][:], in1=centred[:, :, cols], op=ALU.mult)
            nc.sync.dma_start(out=out_view[:, :, cols], in_=result[:])
